import numpy as np, ml_dtypes
CORES = [1,129,9,137,57,185,105,233,113,241,121,249]
N = 12
S, B = 2, 512
def setup_inputs(rng):
    return {"x": rng.standard_normal((N, 128, S * B), dtype=np.float32).astype(ml_dtypes.bfloat16), "gate": (0.9375 + 0.03125 * rng.standard_normal((N, 128, S * B), dtype=np.float32)).astype(ml_dtypes.bfloat16)}
def setup_inputs_big(rng):
    d = setup_inputs(rng)
    for k in ("x",): d[k] = (d[k].astype(np.float32) * 1048576.0).astype(d[k].dtype)
    return d
def setup_inputs_small(rng):
    d = setup_inputs(rng)
    for k in ("x",): d[k] = (d[k].astype(np.float32) * (1 / 1048576.0)).astype(d[k].dtype)
    return d
def setup_inputs_apart(rng):
    d = setup_inputs(rng)
    f = (10.0 ** rng.permutation(np.linspace(-1.5, 1.5, N))).astype(np.float32).reshape(N, 1, 1)
    for k in ("x",): d[k] = (d[k].astype(np.float32) * f).astype(d[k].dtype)
    return d
def reference(x, gate):
    X, GATE = x.astype(np.float64), gate.astype(np.float64)
    y = np.zeros((N, 128, S * B)); h = np.zeros((128, B))
    for r in range(N):
        for s in range(S):
            h = GATE[r][:, B * s:B * s + B] * h + X[r][:, B * s:B * s + B]
            y[r][:, B * s:B * s + B] = h
    return {"y": y.astype(ml_dtypes.bfloat16)}

@@ -1,0 +1,208 @@
+from concourse.bass import DstId, RemoteDMATransfer
+from concourse.mybir import AluOpType
+
+NSIM = 256
+N, B = 12, 512
+W = 8
+C = B // W
+G = 4
+WG = W // G
+HGROUPS = [[1, 2], [3, 4, 5, 6], [7, 8, 9, 10]]
+
+SCRATCH = {
+    "gbuf": ("sbuf", [128, 2, W, C], "bfloat16"),
+    "xbuf": ("sbuf", [128, 2, W, C], "bfloat16"),
+    "ab": ("sbuf", [128, W, 2, C], "bfloat16"),
+    "bz": ("sbuf", [128, W, C], "bfloat16"),
+    "land": ("sbuf", [128, N - 1, 2, C], "bfloat16"),
+    "land0": ("sbuf", [128, C], "bfloat16"),
+    "hs": ("sbuf", [128, N - 1, C], "bfloat16"),
+    "hin": ("sbuf", [128, W, C], "bfloat16"),
+    "t2": ("sbuf", [128, 2, W, C], "float32"),
+    "ybuf": ("sbuf", [128, 2, W, C], "bfloat16"),
+    "tps": ("psum", [128, W, C], "float32"),
+    "cp0": ("psum", [128, W, C], "float32"),
+    "cp1": ("psum", [128, W, C], "float32"),
+    "lp0": ("psum", [128, W, C], "float32"),
+    "lp1": ("psum", [128, W, C], "float32"),
+}
+SEMAPHORES = (["ldg", "ldx", "va", "vt", "pre", "f0", "f1", "yd0", "yd1", "st", "loc", "rl", "hin", "vp"]
+              + ["vb%d" % k for k in range(G)] + ["src%d" % r for r in range(N - 1)] + ["h%d" % r for r in range(1, N - 1)])
+
+
+def _bits(m):
+    return [i for i in range(m.bit_length()) if (m >> i) & 1]
+
+
+def _masks(topo, src, dsts):
+    common = topo.mask(src, dsts[0])
+    for d in dsts:
+        common &= topo.mask(src, d)
+    bits = _bits(common)
+    per = 1
+    while per * 2 * len(dsts) <= len(bits):
+        per *= 2
+    out = []
+    for i in range(len(dsts)):
+        m = 0
+        for b in bits[i * per:(i + 1) * per]:
+            m |= 1 << b
+        out.append(m)
+    return out
+
+
+def _count(topo, src, dsts, dst):
+    return len(_bits(_masks(topo, src, dsts)[dsts.index(dst)]))
+
+
+def _chip_cores(topo, core):
+    return [c for c in range(NSIM) if topo.host(c) == topo.host(core) and topo.chip(c) == topo.chip(core)]
+
+
+def _plan(T, topo):
+    cores = list(T.cores)
+    one = [r for r in range(N) if r == 0 or topo.same_plane(cores[0], cores[r])]
+    two = [r for r in range(N) if r not in one]
+    big, small = (one, two) if len(one) >= len(two) else (two, one)
+    workers = []
+    for r in big[:W]:
+        cand = [c for c in _chip_cores(topo, cores[r]) if c not in cores and topo.die(c) == topo.die(cores[r])
+                and all(topo.may_write(c, d) for d in cores)]
+        workers.append(cand[0])
+    relays, relay_of = {}, {}
+    for r in small:
+        if r < N - 1:
+            cand = [c for c in _chip_cores(topo, cores[r]) if c not in cores and all(topo.may_write(c, w) for w in workers)]
+            relays[r] = cand[:G]
+            for k, c in enumerate(relays[r]):
+                relay_of[c] = (r, k)
+    return {"cores": cores, "big": big, "workers": workers, "relays": relays, "relay_of": relay_of}
+
+
+def _send(g, T, topo, core, items):
+    dsts = [it[0] for it in items]
+    masks = _masks(topo, core, dsts)
+    trs, total = [], 0
+    for (d, src, dst, sem), m in zip(items, masks):
+        rid, pid = topo.addr(d, core)
+        trs.append(RemoteDMATransfer(dst_ids=[DstId(rid=rid, pnc=pid)], dma_engine_mask=m, remote_sem=sem, src=src, dst=dst))
+        total += len(_bits(m))
+    g.remote_dma_fused(trs, local_sem=T.sem.loc)
+    return total
+
+
+def _rank(g, core, T, topo, pl, r):
+    v, S = g.vector, T.sem
+    mult, add = AluOpType.mult, AluOpType.add
+    cores, workers = pl["cores"], pl["workers"]
+    first = r == 0
+    order = [(k + r) % G for k in range(G)]
+    if first:
+        g.sync.dma_start(out=T.gbuf[:, 1], in_=T.gate[:, B:2 * B]).then_inc(S.ldg, 16)
+        g.sync.dma_start(out=T.y[:, 0:B], in_=T.x[:, 0:B]).then_inc(S.st, 16)
+    else:
+        g.sync.dma_start(out=T.gbuf[:], in_=T.gate[:]).then_inc(S.ldg, 16)
+    g.scalar.dma_start(out=T.xbuf[:], in_=T.x[:]).then_inc(S.ldx, 16)
+    v.wait_ge(S.ldg, 16)
+    if not first:
+        v.tensor_tensor(out=T.ab[:, :, 0, :], in0=T.gbuf[:, 0], in1=T.gbuf[:, 1], op=mult).then_inc(S.va, 1)
+    v.wait_ge(S.ldx, 16)
+    for i, k in enumerate(order):
+        a, b = k * WG, (k + 1) * WG
+        v.tensor_tensor(out=T.tps[:, a:b, :], in0=T.gbuf[:, 1, a:b, :], in1=T.xbuf[:, 0, a:b, :], op=mult).then_inc(S.vt, 1)
+        if i == 0 and not first:
+            v.wait_ge(S.va, 1)
+        v.wait_ge(S.vt, i + 1)
+        out = T.bz[:, a:b, :] if first else T.ab[:, a:b, 1, :]
+        v.tensor_tensor(out=out, in0=T.tps[:, a:b, :], in1=T.xbuf[:, 1, a:b, :], op=add).then_inc(S["vb%d" % k], 1)
+    loc = 0
+    if r < N - 1:
+        for k in order:
+            a, b = k * WG, (k + 1) * WG
+            g.wait_ge(S["vb%d" % k], 1)
+            if r in pl["big"]:
+                loc += _send(g, T, topo, core, [(workers[j], T.ab[:, j], T.land[:, r], S["src%d" % r]) for j in range(a, b)])
+            elif first:
+                loc += _send(g, T, topo, core, [(pl["relays"][r][k], T.bz[:, a:b], T.bz[:, a:b], S.rl)])
+            else:
+                loc += _send(g, T, topo, core, [(pl["relays"][r][k], T.ab[:, a:b], T.ab[:, a:b], S.rl)])
+    if first:
+        loc += _send(g, T, topo, core, [(cores[1], T.bz[:], T.hin[:], S.hin)])
+        for k in range(G):
+            g.scalar.wait_ge(S["vb%d" % k], 1)
+        g.scalar.dma_start(out=T.y[:, B:2 * B], in_=T.bz[:]).then_inc(S.st, 16)
+    else:
+        v.tensor_copy(out=T.cp0[:], in_=T.gbuf[:, 0]).then_inc(S.pre, 1)
+        v.tensor_copy(out=T.lp0[:], in_=T.xbuf[:, 0]).then_inc(S.pre, 1)
+        for k in range(G):
+            v.wait_ge(S["vb%d" % k], 1)
+        v.tensor_copy(out=T.cp1[:], in_=T.ab[:, :, 0, :]).then_inc(S.pre, 1)
+        v.tensor_copy(out=T.lp1[:], in_=T.ab[:, :, 1, :]).then_inc(S.pre, 1)
+        v.wait_ge(S.pre, 4)
+        if r == 1:
+            nh = _count(topo, cores[0], [cores[1]], cores[1])
+        else:
+            grp = [q for q in HGROUPS if r - 1 in q][0]
+            nh = sum(_count(topo, w, [cores[q + 1] for q in grp], core) for w in workers)
+        v.wait_ge(S.hin, nh)
+        v.tensor_tensor(out=T.t2[:, 0], in0=T.cp0[:], in1=T.hin[:], op=mult).then_inc(S.f0, 1)
+        v.tensor_tensor(out=T.t2[:, 1], in0=T.cp1[:], in1=T.hin[:], op=mult).then_inc(S.f1, 1)
+        v.wait_ge(S.f0, 1)
+        v.tensor_tensor(out=T.ybuf[:, 0], in0=T.lp0[:], in1=T.t2[:, 0], op=add).then_inc(S.yd0, 1)
+        v.wait_ge(S.f1, 1)
+        v.tensor_tensor(out=T.ybuf[:, 1], in0=T.lp1[:], in1=T.t2[:, 1], op=add).then_inc(S.yd1, 1)
+        g.sync.wait_ge(S.yd0, 1)
+        g.sync.dma_start(out=T.y[:, 0:B], in_=T.ybuf[:, 0]).then_inc(S.st, 16)
+        g.scalar.wait_ge(S.yd1, 1)
+        g.scalar.dma_start(out=T.y[:, B:2 * B], in_=T.ybuf[:, 1]).then_inc(S.st, 16)
+    if loc:
+        g.wait_ge(S.loc, loc)
+    g.wait_ge(S.st, 32)
+
+
+def _relay(g, core, T, topo, pl):
+    S = T.sem
+    r, k = pl["relay_of"][core]
+    g.wait_ge(S.rl, _count(topo, pl["cores"][r], [core], core))
+    items = []
+    for j in range(k * WG, (k + 1) * WG):
+        if r == 0:
+            items.append((pl["workers"][j], T.bz[:, j], T.land0[:], S.src0))
+        else:
+            items.append((pl["workers"][j], T.ab[:, j], T.land[:, r], S["src%d" % r]))
+    g.wait_ge(S.loc, _send(g, T, topo, core, items))
+
+
+def _worker(g, core, T, topo, pl):
+    v, S = g.vector, T.sem
+    cores, workers = pl["cores"], pl["workers"]
+    j = workers.index(core)
+    k = j // WG
+    peers = workers[k * WG:(k + 1) * WG]
+    prev = T.land0[:]
+    for r in range(N - 1):
+        sender = cores[r] if r in pl["big"] else pl["relays"][r][k]
+        v.wait_ge(S["src%d" % r], _count(topo, sender, peers, core))
+        if r == 0:
+            continue
+        v.tensor_tensor(out=T.tps[:, 0, :], in0=T.land[:, r, 0, :], in1=prev, op=AluOpType.mult).then_inc(S.vp, 1)
+        v.wait_ge(S.vp, r)
+        v.tensor_tensor(out=T.hs[:, r, :], in0=T.tps[:, 0, :], in1=T.land[:, r, 1, :], op=AluOpType.add).then_inc(S["h%d" % r], 1)
+        v.wait_ge(S["h%d" % r], 1)
+        prev = T.hs[:, r, :]
+    loc = 0
+    for grp in HGROUPS:
+        g.wait_ge(S["h%d" % grp[-1]], 1)
+        loc += _send(g, T, topo, core, [(cores[q + 1], T.hs[:, q, :], T.hin[:, j, :], S.hin) for q in grp])
+    g.wait_ge(S.loc, loc)
+
+
+def rank_program(g, core, T, topo):
+    pl = _plan(T, topo)
+    rank = T.rank_of(core)
+    if rank is not None:
+        _rank(g, core, T, topo, pl, rank)
+    elif core in pl["workers"]:
+        _worker(g, core, T, topo, pl)
+    elif core in pl["relay_of"]:
+        _relay(g, core, T, topo, pl)

@@ -1,5 +1,5 @@
 from concourse.bass import DstId, RemoteDMATransfer
-from concourse.mybir import AluOpType
+from concourse.mybir import AluOpType, ActivationFunctionType
 
 NSIM = 256
 N, B = 12, 512
@@ -7,6 +7,7 @@ W = 8
 C = B // W
 G = 4
 WG = W // G
+R = N - 1
 HGROUPS = [[1, 2], [3, 4, 5, 6], [7, 8, 9, 10]]
 
 SCRATCH = {
@@ -16,6 +17,8 @@ SCRATCH = {
     "bz": ("sbuf", [128, W, C], "bfloat16"),
     "land": ("sbuf", [128, N - 1, 2, C], "bfloat16"),
     "land0": ("sbuf", [128, C], "bfloat16"),
+    "il": ("sbuf", [128, 2, C * R], "bfloat16"),
+    "ho": ("sbuf", [128, C * R], "bfloat16"),
     "hs": ("sbuf", [128, N - 1, C], "bfloat16"),
     "hin": ("sbuf", [128, W, C], "bfloat16"),
     "t2": ("sbuf", [128, 2, W, C], "float32"),
@@ -26,7 +29,7 @@ SCRATCH = {
     "lp0": ("psum", [128, W, C], "float32"),
     "lp1": ("psum", [128, W, C], "float32"),
 }
-SEMAPHORES = (["ldg", "ldx", "va", "vt", "pre", "f0", "f1", "yd0", "yd1", "st", "loc", "rl", "hin", "vp"]
+SEMAPHORES = (["ldg", "ldx", "va", "vt", "pre", "f0", "f1", "yd0", "yd1", "st", "loc", "rl", "hin", "il", "sc"]
               + ["vb%d" % k for k in range(G)] + ["src%d" % r for r in range(N - 1)] + ["h%d" % r for r in range(1, N - 1)])
 
 
@@ -34,9 +37,9 @@ def _bits(m):
     return [i for i in range(m.bit_length()) if (m >> i) & 1]
 
 
-def _masks(topo, src, dsts):
+def _masks(topo, src, dsts, also=()):
     common = topo.mask(src, dsts[0])
-    for d in dsts:
+    for d in list(dsts) + [c for c in also if c != src]:
         common &= topo.mask(src, d)
     bits = _bits(common)
     per = 1
@@ -51,8 +54,8 @@ def _masks(topo, src, dsts):
     return out
 
 
-def _count(topo, src, dsts, dst):
-    return len(_bits(_masks(topo, src, dsts)[dsts.index(dst)]))
+def _count(topo, src, dsts, dst, also=()):
+    return len(_bits(_masks(topo, src, dsts, also)[dsts.index(dst)]))
 
 
 def _chip_cores(topo, core):
@@ -64,24 +67,45 @@ def _plan(T, topo):
     one = [r for r in range(N) if r == 0 or topo.same_plane(cores[0], cores[r])]
     two = [r for r in range(N) if r not in one]
     big, small = (one, two) if len(one) >= len(two) else (two, one)
-    workers = []
-    for r in big[:W]:
+    senders = [r for r in big if r < N - 1]
+    lastbig = senders[-1]
+    workers, home = [], []
+    for r in senders[:W]:
         cand = [c for c in _chip_cores(topo, cores[r]) if c not in cores and topo.die(c) == topo.die(cores[r])
                 and all(topo.may_write(c, d) for d in cores)]
         workers.append(cand[0])
-    relays, relay_of = {}, {}
+        home.append(r)
+    spare = [c for c in _chip_cores(topo, cores[lastbig]) if c not in cores and c not in workers
+             and all(topo.may_write(c, d) for d in cores)]
+    spare.sort(key=lambda c: topo.die(c) == topo.die(cores[lastbig]))
+    while len(workers) < W:
+        workers.append(spare.pop(0))
+        home.append(lastbig)
+    send = {r: {k: cores[r] for k in range(G)} for r in range(N - 1)}
+    relay_of, order = {}, {}
     for r in small:
         if r < N - 1:
             cand = [c for c in _chip_cores(topo, cores[r]) if c not in cores and all(topo.may_write(c, w) for w in workers)]
-            relays[r] = cand[:G]
-            for k, c in enumerate(relays[r]):
+            for k, c in enumerate(cand[:G]):
+                send[r][k] = c
                 relay_of[c] = (r, k)
-    return {"cores": cores, "big": big, "workers": workers, "relays": relays, "relay_of": relay_of}
+            order[r] = [(k + small.index(r)) % G for k in range(G)]
+    for j, r in enumerate(home):
+        for i in range(G - 1):
+            k = (j // WG + 1 + (j % WG + i) % (G - 1)) % G
+            if send[r][k] == cores[r]:
+                send[r][k] = workers[j]
+                relay_of[workers[j]] = (r, k)
+                break
+    for r in senders:
+        rot = [(k + min(q for q in range(G) if send[r][q] != cores[r])) % G for k in range(G)]
+        order[r] = [k for k in rot if send[r][k] != cores[r]] + [k for k in rot if send[r][k] == cores[r]]
+    return {"cores": cores, "big": big, "workers": workers, "send": send, "relay_of": relay_of, "order": order}
 
 
-def _send(g, T, topo, core, items):
+def _send(g, T, topo, core, items, also=()):
     dsts = [it[0] for it in items]
-    masks = _masks(topo, core, dsts)
+    masks = _masks(topo, core, dsts, also)
     trs, total = [], 0
     for (d, src, dst, sem), m in zip(items, masks):
         rid, pid = topo.addr(d, core)
@@ -91,12 +115,16 @@ def _send(g, T, topo, core, items):
     return total
 
 
+def _also(pl, r):
+    return pl["workers"] if r in pl["big"] else ()
+
+
 def _rank(g, core, T, topo, pl, r):
     v, S = g.vector, T.sem
     mult, add = AluOpType.mult, AluOpType.add
     cores, workers = pl["cores"], pl["workers"]
     first = r == 0
-    order = [(k + r) % G for k in range(G)]
+    order = pl["order"][r] if r < N - 1 else list(range(G))
     if first:
         g.sync.dma_start(out=T.gbuf[:, 1], in_=T.gate[:, B:2 * B]).then_inc(S.ldg, 16)
         g.sync.dma_start(out=T.y[:, 0:B], in_=T.x[:, 0:B]).then_inc(S.st, 16)
@@ -120,12 +148,14 @@ def _rank(g, core, T, topo, pl, r):
         for k in order:
             a, b = k * WG, (k + 1) * WG
             g.wait_ge(S["vb%d" % k], 1)
-            if r in pl["big"]:
-                loc += _send(g, T, topo, core, [(workers[j], T.ab[:, j], T.land[:, r], S["src%d" % r]) for j in range(a, b)])
+            via = pl["send"][r][k]
+            if via == core:
+                loc += _send(g, T, topo, core,
+                             [(workers[j], T.ab[:, j], T.land[:, r], S["src%d" % r]) for j in range(a, b)], workers)
             elif first:
-                loc += _send(g, T, topo, core, [(pl["relays"][r][k], T.bz[:, a:b], T.bz[:, a:b], S.rl)])
+                loc += _send(g, T, topo, core, [(via, T.bz[:, a:b], T.bz[:, a:b], S.rl)])
             else:
-                loc += _send(g, T, topo, core, [(pl["relays"][r][k], T.ab[:, a:b], T.ab[:, a:b], S.rl)])
+                loc += _send(g, T, topo, core, [(via, T.ab[:, a:b], T.ab[:, a:b], S.rl)], _also(pl, r))
     if first:
         loc += _send(g, T, topo, core, [(cores[1], T.bz[:], T.hin[:], S.hin)])
         for k in range(G):
@@ -160,39 +190,55 @@ def _rank(g, core, T, topo, pl, r):
     g.wait_ge(S.st, 32)
 
 
-def _relay(g, core, T, topo, pl):
+def _pass_on(g, core, T, topo, pl):
     S = T.sem
     r, k = pl["relay_of"][core]
-    g.wait_ge(S.rl, _count(topo, pl["cores"][r], [core], core))
+    g.wait_ge(S.rl, _count(topo, pl["cores"][r], [core], core, _also(pl, r)))
     items = []
     for j in range(k * WG, (k + 1) * WG):
         if r == 0:
             items.append((pl["workers"][j], T.bz[:, j], T.land0[:], S.src0))
         else:
             items.append((pl["workers"][j], T.ab[:, j], T.land[:, r], S["src%d" % r]))
-    g.wait_ge(S.loc, _send(g, T, topo, core, items))
+    return _send(g, T, topo, core, items, pl["workers"])
 
 
 def _worker(g, core, T, topo, pl):
-    v, S = g.vector, T.sem
+    v, sc, S = g.vector, g.scalar, T.sem
     cores, workers = pl["cores"], pl["workers"]
     j = workers.index(core)
     k = j // WG
     peers = workers[k * WG:(k + 1) * WG]
-    prev = T.land0[:]
-    for r in range(N - 1):
-        sender = cores[r] if r in pl["big"] else pl["relays"][r][k]
-        v.wait_ge(S["src%d" % r], _count(topo, sender, peers, core))
-        if r == 0:
-            continue
-        v.tensor_tensor(out=T.tps[:, 0, :], in0=T.land[:, r, 0, :], in1=prev, op=AluOpType.mult).then_inc(S.vp, 1)
-        v.wait_ge(S.vp, r)
-        v.tensor_tensor(out=T.hs[:, r, :], in0=T.tps[:, 0, :], in1=T.land[:, r, 1, :], op=AluOpType.add).then_inc(S["h%d" % r], 1)
-        v.wait_ge(S["h%d" % r], 1)
-        prev = T.hs[:, r, :]
-    loc = 0
+    loc = _pass_on(g, core, T, topo, pl) if core in pl["relay_of"] else 0
+    v.memset(T.il[:, 0, 0::R], 0.0).then_inc(S.il, 1)
+    nil = 1 + R
+    straight = sorted([r for r in range(R) if pl["send"][r][k] == cores[r]], key=lambda r: (pl["order"][r].index(k), r))
+    passed = sorted([r for r in range(R) if pl["send"][r][k] != cores[r]], key=lambda r: (pl["order"][r].index(k), r))
+    for r in straight:
+        v.wait_ge(S["src%d" % r], _count(topo, pl["send"][r][k], peers, core, workers))
+        if r > 0:
+            v.tensor_copy(out=T.il[:, :, r::R], in_=T.land[:, r]).then_inc(S.il, 1)
+        else:
+            v.tensor_copy(out=T.il[:, 1, r::R], in_=T.land0[:]).then_inc(S.il, 1)
+    for r in passed:
+        sc.wait_ge(S["src%d" % r], _count(topo, pl["send"][r][k], peers, core, workers))
+        if r > 0:
+            sc.activation(out=T.il[:, :, r::R], in_=T.land[:, r], func=ActivationFunctionType.Copy).then_inc(S.il, 1)
+        else:
+            sc.activation(out=T.il[:, 1, r::R], in_=T.land0[:], func=ActivationFunctionType.Copy).then_inc(S.il, 1)
+    v.wait_ge(S.il, nil)
+    v.tensor_tensor_scan(out=T.ho[:], data0=T.il[:, 0, :], data1=T.il[:, 1, :], initial=0.0,
+                         op0=AluOpType.mult, op1=AluOpType.add).then_inc(S.sc, 1)
+    v.wait_ge(S.sc, 1)
+    sc.wait_ge(S.sc, 1)
+    for r in range(1, R):
+        if r % 2:
+            v.tensor_copy(out=T.hs[:, r, :], in_=T.ho[:, r::R]).then_inc(S["h%d" % r], 1)
+        else:
+            sc.activation(out=T.hs[:, r, :], in_=T.ho[:, r::R], func=ActivationFunctionType.Copy).then_inc(S["h%d" % r], 1)
     for grp in HGROUPS:
-        g.wait_ge(S["h%d" % grp[-1]], 1)
+        for q in grp:
+            g.wait_ge(S["h%d" % q], 1)
         loc += _send(g, T, topo, core, [(cores[q + 1], T.hs[:, q, :], T.hin[:, j, :], S.hin) for q in grp])
     g.wait_ge(S.loc, loc)
 
@@ -205,4 +251,4 @@ def rank_program(g, core, T, topo):
     elif core in pl["workers"]:
         _worker(g, core, T, topo, pl)
     elif core in pl["relay_of"]:
-        _relay(g, core, T, topo, pl)
+        g.wait_ge(T.sem.loc, _pass_on(g, core, T, topo, pl))

from concourse.bass import DstId, RemoteDMATransfer
from concourse.mybir import AluOpType, ActivationFunctionType

NSIM = 256
N, B = 12, 512
W = 8
C = B // W
G = 4
WG = W // G
R = N - 1
HGROUPS = [[1, 2], [3, 4, 5, 6], [7, 8, 9, 10]]

SCRATCH = {
    "gbuf": ("sbuf", [128, 2, W, C], "bfloat16"),
    "xbuf": ("sbuf", [128, 2, W, C], "bfloat16"),
    "ab": ("sbuf", [128, W, 2, C], "bfloat16"),
    "bz": ("sbuf", [128, W, C], "bfloat16"),
    "land": ("sbuf", [128, N - 1, 2, C], "bfloat16"),
    "land0": ("sbuf", [128, C], "bfloat16"),
    "il": ("sbuf", [128, 2, C * R], "bfloat16"),
    "ho": ("sbuf", [128, C * R], "bfloat16"),
    "hs": ("sbuf", [128, N - 1, C], "bfloat16"),
    "hin": ("sbuf", [128, W, C], "bfloat16"),
    "t2": ("sbuf", [128, 2, W, C], "float32"),
    "ybuf": ("sbuf", [128, 2, W, C], "bfloat16"),
    "tps": ("psum", [128, W, C], "float32"),
    "cp0": ("psum", [128, W, C], "float32"),
    "cp1": ("psum", [128, W, C], "float32"),
    "lp0": ("psum", [128, W, C], "float32"),
    "lp1": ("psum", [128, W, C], "float32"),
}
SEMAPHORES = (["ldg", "ldx", "va", "vt", "pre", "f0", "f1", "yd0", "yd1", "st", "loc", "rl", "hin", "il", "sc"]
              + ["vb%d" % k for k in range(G)] + ["src%d" % r for r in range(N - 1)] + ["h%d" % r for r in range(1, N - 1)])


def _bits(m):
    return [i for i in range(m.bit_length()) if (m >> i) & 1]


def _masks(topo, src, dsts, also=()):
    common = topo.mask(src, dsts[0])
    for d in list(dsts) + [c for c in also if c != src]:
        common &= topo.mask(src, d)
    bits = _bits(common)
    per = 1
    while per * 2 * len(dsts) <= len(bits):
        per *= 2
    out = []
    for i in range(len(dsts)):
        m = 0
        for b in bits[i * per:(i + 1) * per]:
            m |= 1 << b
        out.append(m)
    return out


def _count(topo, src, dsts, dst, also=()):
    return len(_bits(_masks(topo, src, dsts, also)[dsts.index(dst)]))


def _chip_cores(topo, core):
    return [c for c in range(NSIM) if topo.host(c) == topo.host(core) and topo.chip(c) == topo.chip(core)]


def _plan(T, topo):
    cores = list(T.cores)
    one = [r for r in range(N) if r == 0 or topo.same_plane(cores[0], cores[r])]
    two = [r for r in range(N) if r not in one]
    big, small = (one, two) if len(one) >= len(two) else (two, one)
    senders = [r for r in big if r < N - 1]
    lastbig = senders[-1]
    workers, home = [], []
    for r in senders[:W]:
        cand = [c for c in _chip_cores(topo, cores[r]) if c not in cores and topo.die(c) == topo.die(cores[r])
                and all(topo.may_write(c, d) for d in cores)]
        workers.append(cand[0])
        home.append(r)
    spare = [c for c in _chip_cores(topo, cores[lastbig]) if c not in cores and c not in workers
             and all(topo.may_write(c, d) for d in cores)]
    spare.sort(key=lambda c: topo.die(c) == topo.die(cores[lastbig]))
    while len(workers) < W:
        workers.append(spare.pop(0))
        home.append(lastbig)
    send = {r: {k: cores[r] for k in range(G)} for r in range(N - 1)}
    relay_of, order = {}, {}
    for r in small:
        if r < N - 1:
            cand = [c for c in _chip_cores(topo, cores[r]) if c not in cores and all(topo.may_write(c, w) for w in workers)]
            for k, c in enumerate(cand[:G]):
                send[r][k] = c
                relay_of[c] = (r, k)
            order[r] = [(k + small.index(r)) % G for k in range(G)]
    for j, r in enumerate(home):
        for i in range(G - 1):
            k = (j // WG + 1 + (j % WG + i) % (G - 1)) % G
            if send[r][k] == cores[r]:
                send[r][k] = workers[j]
                relay_of[workers[j]] = (r, k)
                break
    for r in senders:
        rot = [(k + min(q for q in range(G) if send[r][q] != cores[r])) % G for k in range(G)]
        order[r] = [k for k in rot if send[r][k] != cores[r]] + [k for k in rot if send[r][k] == cores[r]]
    return {"cores": cores, "big": big, "workers": workers, "send": send, "relay_of": relay_of, "order": order}


def _send(g, T, topo, core, items, also=()):
    dsts = [it[0] for it in items]
    masks = _masks(topo, core, dsts, also)
    trs, total = [], 0
    for (d, src, dst, sem), m in zip(items, masks):
        rid, pid = topo.addr(d, core)
        trs.append(RemoteDMATransfer(dst_ids=[DstId(rid=rid, pnc=pid)], dma_engine_mask=m, remote_sem=sem, src=src, dst=dst))
        total += len(_bits(m))
    g.remote_dma_fused(trs, local_sem=T.sem.loc)
    return total


def _also(pl, r):
    return pl["workers"] if r in pl["big"] else ()


def _rank(g, core, T, topo, pl, r):
    v, S = g.vector, T.sem
    mult, add = AluOpType.mult, AluOpType.add
    cores, workers = pl["cores"], pl["workers"]
    first = r == 0
    order = pl["order"][r] if r < N - 1 else list(range(G))
    if first:
        g.sync.dma_start(out=T.gbuf[:, 1], in_=T.gate[:, B:2 * B]).then_inc(S.ldg, 16)
        g.sync.dma_start(out=T.y[:, 0:B], in_=T.x[:, 0:B]).then_inc(S.st, 16)
    else:
        g.sync.dma_start(out=T.gbuf[:], in_=T.gate[:]).then_inc(S.ldg, 16)
    g.scalar.dma_start(out=T.xbuf[:], in_=T.x[:]).then_inc(S.ldx, 16)
    v.wait_ge(S.ldg, 16)
    if not first:
        v.tensor_tensor(out=T.ab[:, :, 0, :], in0=T.gbuf[:, 0], in1=T.gbuf[:, 1], op=mult).then_inc(S.va, 1)
    v.wait_ge(S.ldx, 16)
    for i, k in enumerate(order):
        a, b = k * WG, (k + 1) * WG
        v.tensor_tensor(out=T.tps[:, a:b, :], in0=T.gbuf[:, 1, a:b, :], in1=T.xbuf[:, 0, a:b, :], op=mult).then_inc(S.vt, 1)
        if i == 0 and not first:
            v.wait_ge(S.va, 1)
        v.wait_ge(S.vt, i + 1)
        out = T.bz[:, a:b, :] if first else T.ab[:, a:b, 1, :]
        v.tensor_tensor(out=out, in0=T.tps[:, a:b, :], in1=T.xbuf[:, 1, a:b, :], op=add).then_inc(S["vb%d" % k], 1)
    loc = 0
    if r < N - 1:
        for k in order:
            a, b = k * WG, (k + 1) * WG
            g.wait_ge(S["vb%d" % k], 1)
            via = pl["send"][r][k]
            if via == core:
                loc += _send(g, T, topo, core,
                             [(workers[j], T.ab[:, j], T.land[:, r], S["src%d" % r]) for j in range(a, b)], workers)
            elif first:
                loc += _send(g, T, topo, core, [(via, T.bz[:, a:b], T.bz[:, a:b], S.rl)])
            else:
                loc += _send(g, T, topo, core, [(via, T.ab[:, a:b], T.ab[:, a:b], S.rl)], _also(pl, r))
    if first:
        loc += _send(g, T, topo, core, [(cores[1], T.bz[:], T.hin[:], S.hin)])
        for k in range(G):
            g.scalar.wait_ge(S["vb%d" % k], 1)
        g.scalar.dma_start(out=T.y[:, B:2 * B], in_=T.bz[:]).then_inc(S.st, 16)
    else:
        v.tensor_copy(out=T.cp0[:], in_=T.gbuf[:, 0]).then_inc(S.pre, 1)
        v.tensor_copy(out=T.lp0[:], in_=T.xbuf[:, 0]).then_inc(S.pre, 1)
        for k in range(G):
            v.wait_ge(S["vb%d" % k], 1)
        v.tensor_copy(out=T.cp1[:], in_=T.ab[:, :, 0, :]).then_inc(S.pre, 1)
        v.tensor_copy(out=T.lp1[:], in_=T.ab[:, :, 1, :]).then_inc(S.pre, 1)
        v.wait_ge(S.pre, 4)
        if r == 1:
            nh = _count(topo, cores[0], [cores[1]], cores[1])
        else:
            grp = [q for q in HGROUPS if r - 1 in q][0]
            nh = sum(_count(topo, w, [cores[q + 1] for q in grp], core) for w in workers)
        v.wait_ge(S.hin, nh)
        v.tensor_tensor(out=T.t2[:, 0], in0=T.cp0[:], in1=T.hin[:], op=mult).then_inc(S.f0, 1)
        v.tensor_tensor(out=T.t2[:, 1], in0=T.cp1[:], in1=T.hin[:], op=mult).then_inc(S.f1, 1)
        v.wait_ge(S.f0, 1)
        v.tensor_tensor(out=T.ybuf[:, 0], in0=T.lp0[:], in1=T.t2[:, 0], op=add).then_inc(S.yd0, 1)
        v.wait_ge(S.f1, 1)
        v.tensor_tensor(out=T.ybuf[:, 1], in0=T.lp1[:], in1=T.t2[:, 1], op=add).then_inc(S.yd1, 1)
        g.sync.wait_ge(S.yd0, 1)
        g.sync.dma_start(out=T.y[:, 0:B], in_=T.ybuf[:, 0]).then_inc(S.st, 16)
        g.scalar.wait_ge(S.yd1, 1)
        g.scalar.dma_start(out=T.y[:, B:2 * B], in_=T.ybuf[:, 1]).then_inc(S.st, 16)
    if loc:
        g.wait_ge(S.loc, loc)
    g.wait_ge(S.st, 32)


def _pass_on(g, core, T, topo, pl):
    S = T.sem
    r, k = pl["relay_of"][core]
    g.wait_ge(S.rl, _count(topo, pl["cores"][r], [core], core, _also(pl, r)))
    items = []
    for j in range(k * WG, (k + 1) * WG):
        if r == 0:
            items.append((pl["workers"][j], T.bz[:, j], T.land0[:], S.src0))
        else:
            items.append((pl["workers"][j], T.ab[:, j], T.land[:, r], S["src%d" % r]))
    return _send(g, T, topo, core, items, pl["workers"])


def _worker(g, core, T, topo, pl):
    v, sc, S = g.vector, g.scalar, T.sem
    cores, workers = pl["cores"], pl["workers"]
    j = workers.index(core)
    k = j // WG
    peers = workers[k * WG:(k + 1) * WG]
    loc = _pass_on(g, core, T, topo, pl) if core in pl["relay_of"] else 0
    v.memset(T.il[:, 0, 0::R], 0.0).then_inc(S.il, 1)
    nil = 1 + R
    straight = sorted([r for r in range(R) if pl["send"][r][k] == cores[r]], key=lambda r: (pl["order"][r].index(k), r))
    passed = sorted([r for r in range(R) if pl["send"][r][k] != cores[r]], key=lambda r: (pl["order"][r].index(k), r))
    for r in straight:
        v.wait_ge(S["src%d" % r], _count(topo, pl["send"][r][k], peers, core, workers))
        if r > 0:
            v.tensor_copy(out=T.il[:, :, r::R], in_=T.land[:, r]).then_inc(S.il, 1)
        else:
            v.tensor_copy(out=T.il[:, 1, r::R], in_=T.land0[:]).then_inc(S.il, 1)
    for r in passed:
        sc.wait_ge(S["src%d" % r], _count(topo, pl["send"][r][k], peers, core, workers))
        if r > 0:
            sc.activation(out=T.il[:, :, r::R], in_=T.land[:, r], func=ActivationFunctionType.Copy).then_inc(S.il, 1)
        else:
            sc.activation(out=T.il[:, 1, r::R], in_=T.land0[:], func=ActivationFunctionType.Copy).then_inc(S.il, 1)
    v.wait_ge(S.il, nil)
    v.tensor_tensor_scan(out=T.ho[:], data0=T.il[:, 0, :], data1=T.il[:, 1, :], initial=0.0,
                         op0=AluOpType.mult, op1=AluOpType.add).then_inc(S.sc, 1)
    v.wait_ge(S.sc, 1)
    sc.wait_ge(S.sc, 1)
    for r in range(1, R):
        if r % 2:
            v.tensor_copy(out=T.hs[:, r, :], in_=T.ho[:, r::R]).then_inc(S["h%d" % r], 1)
        else:
            sc.activation(out=T.hs[:, r, :], in_=T.ho[:, r::R], func=ActivationFunctionType.Copy).then_inc(S["h%d" % r], 1)
    for grp in HGROUPS:
        for q in grp:
            g.wait_ge(S["h%d" % q], 1)
        loc += _send(g, T, topo, core, [(cores[q + 1], T.hs[:, q, :], T.hin[:, j, :], S.hin) for q in grp])
    g.wait_ge(S.loc, loc)


def rank_program(g, core, T, topo):
    pl = _plan(T, topo)
    rank = T.rank_of(core)
    if rank is not None:
        _rank(g, core, T, topo, pl, rank)
    elif core in pl["workers"]:
        _worker(g, core, T, topo, pl)
    elif core in pl["relay_of"]:
        g.wait_ge(T.sem.loc, _pass_on(g, core, T, topo, pl))
